import numpy as np
import ml_dtypes


def mxq(x, axis, fmt="e4m3"):
    dtype, down = {"e4m3": (ml_dtypes.float8_e4m3fn, 7), "e5m2": (ml_dtypes.float8_e5m2, 14)}[fmt]
    v = np.moveaxis(np.asarray(x, np.float32).astype(ml_dtypes.bfloat16).astype(np.float64), axis, -1)
    blocks = v.reshape(v.shape[:-1] + (-1, 32))
    amax = np.abs(blocks).max(-1, keepdims=True)
    byte = np.maximum(np.where(amax > 0, np.frexp(amax)[1] - 1 + 127, 0) - down, 1)
    scale = np.exp2(byte - 127.0)
    codes = (blocks / scale).astype(np.float32).astype(dtype).astype(np.float64)
    return np.moveaxis((codes * scale).reshape(v.shape), -1, axis)


WIDE = False


def mx_kscale(k):
    if not WIDE:
        return np.ones(k)
    levels = np.array([10, -10, 5, -5, 0])
    if k % 512:
        return np.exp2(np.random.permutation(np.resize(levels, k // 32))).repeat(32)
    a = np.empty((k // 512, 16))
    for p in range(k // 512):
        a[p, :8] = np.random.permutation(np.resize(levels, 8))
        for g in range(8):
            far = levels[np.abs(levels - a[p, g]) >= 10]
            a[p, g + 8] = far[np.random.randint(len(far))]
    return np.exp2(a.ravel()).repeat(32)


def f64(x):
    return np.asarray(x).astype(np.float64)


def striped(idx):
    return np.tile(idx.reshape(-1, 16).T, (8, 1)).astype(np.uint16)


def unstriped(offs):
    return offs[:16].T.reshape(-1).astype(np.int64)


def relu(v):
    return np.maximum(v, 0.0)

def planes(y):
    n, m = y.shape
    v = y.astype(np.float32).astype(ml_dtypes.bfloat16).astype(np.float64).reshape(n // 32, 32, m)
    top = np.abs(v).max(1)
    byte = np.clip(np.where(top > 0, np.frexp(top)[1] - 1 + 127 - 7, 1), 1, 254)
    codes = (v * np.exp2(127.0 - byte)[:, None, :]).reshape(n, m).astype(np.float32).astype(ml_dtypes.float8_e4m3fn).view(np.uint8)
    words = codes.reshape(n // 512, 128, 4, m).transpose(0, 1, 3, 2)
    return np.ascontiguousarray(words), np.ascontiguousarray(byte.astype(np.uint8).reshape(n // 512, 16, m))


K, T, S, H = 512, 1024, 512, 512


def setup_inputs():
    n = np.random.standard_normal
    s = mx_kscale(K)[:, None]
    u = mx_kscale(H)
    return {
        "xT": (n((K, T)) * s).astype(np.float32),
        "w1": (n((K, H)) / np.sqrt(2 * K) / s).astype(np.float32),
        "w2": (n((K, H)) / np.sqrt(K) / s * u).astype(np.float32),
        "w3": (n((H, H)) / np.sqrt(2 * H) / u[:, None]).astype(np.float32),
        "offs": striped(np.random.permutation(T)[:S]),
    }


def reference(xT, w1, w2, w3, offs):
    xq = mxq(f64(xT)[:, unstriped(offs)], 0, "e4m3")
    h = relu(mxq(f64(w2), 0, "e4m3").T @ xq)
    out_0 = mxq(f64(w1), 0, "e4m3").T @ xq + mxq(f64(w3), 0, "e4m3").T @ mxq(h, 0, "e4m3")
    return (out_0,) + planes(out_0)

@@ -1,0 +1,139 @@
+from contextlib import ExitStack
+
+import concourse.mybir as mybir
+
+K, T, S, H = 512, 1024, 512, 512
+FLOPS = 3 * 2 * K * H * S
+
+F32 = mybir.dt.float32
+BF16 = mybir.dt.bfloat16
+I32 = mybir.dt.int32
+U32 = mybir.dt.uint32
+U16 = mybir.dt.uint16
+U8 = mybir.dt.uint8
+FP8X4 = mybir.dt.float8_e4m3fn_x4
+ACT = mybir.ActivationFunctionType
+
+P = 128
+PACK = 4
+BLK = 128
+
+
+def tile_picked_lora_relu_lo_kernel(tc, xT, w1, w2, w3, offs, out_0, out_1, out_2):
+    nc = tc.nc
+    with ExitStack() as ctx:
+        sb = ctx.enter_context(tc.tile_pool(name="sb", bufs=1))
+        ps = ctx.enter_context(tc.psum_pool(name="ps", bufs=1))
+
+        offsets = sb.tile([P, S // 16], U16, name="offsets")
+        nc.sync.dma_start(offsets[:], offs)
+        x_rows = xT.rearrange("(p j) t -> p j t", j=PACK)
+        x_raw = [sb.tile([P, T], F32, name=f"x_raw{j}") for j in range(PACK)]
+        for j in range(PACK):
+            nc.sync.dma_start(x_raw[j][:], x_rows[:, j, :])
+        w_raw = {}
+        for name, w in (("w2", w2), ("w1", w1), ("w3", w3)):
+            w_raw[name] = sb.tile([P, PACK, H], F32, name=name + "_raw")
+            nc.sync.dma_start(w_raw[name][:], w.rearrange("(p j) c -> p j c", j=PACK))
+
+        def mx_tiles(name, width):
+            return (sb.tile([P, width], U32, name=name + "_codes", align_bytes=64),
+                    sb.tile([P, width], U8, name=name + "_scales", align_bytes=64))
+
+        def quantize(mx, cols, src):
+            nc.vector.quantize_mx(out=mx[0][:, cols].bitcast(FP8X4), scales=mx[1][:, cols], in_=src)
+
+        def matmul(out, w_mx, t, a_mx, cols, start, stop):
+            wc = slice(t * P, (t + 1) * P)
+            nc.tensor.matmul_mx(out=out, lhsT=w_mx[0][:, wc].bitcast(FP8X4), lhsT_scale=w_mx[1][:, wc],
+                                rhs=a_mx[0][:, cols].bitcast(FP8X4), rhs_scale=a_mx[1][:, cols],
+                                start=start, stop=stop)
+
+        def interleave(copy, dst, src, cols):
+            copy(dst[:].rearrange("p (c i j) -> p c j i", i=4, j=PACK),
+                 src[:, :, cols].rearrange("p j (c i) -> p c j i", i=4))
+
+        def deal(copy, name, t0, nt):
+            dst = sb.tile([P, nt * P * PACK], BF16, name=f"{name}_bf{t0}", align_bytes=64)
+            copy(dst[:].rearrange("p (t m j) -> p m j t", t=nt, j=PACK),
+                 w_raw[name][:].rearrange("p j (m t) -> p m j t", t=PACK)[:, :, :, t0:t0 + nt])
+            return dst
+
+        def quantize_w(mx, dst, t0, nt, step):
+            for t in range(0, nt, step):
+                quantize(mx, slice((t0 + t) * P, (t0 + t + step) * P), dst[:, t * P * PACK:(t + step) * P * PACK])
+
+        picked = sb.tile([P, PACK, S], BF16, name="picked")
+        for j in range(PACK - 1):
+            nc.scalar.activation(picked[:, j, :], x_raw[j][:].indirect(offsets[:]), ACT.Copy)
+        half = S // 2
+        j = PACK - 1
+        nc.vector.tensor_copy(picked[:, j, :half], x_raw[j][:].indirect(offsets[:, :half // 16]))
+        nc.scalar.activation(picked[:, j, half:], x_raw[j][:].indirect(offsets[:, half // 16:]), ACT.Copy)
+
+        x_mx = mx_tiles("x", S)
+        x_bf = [sb.tile([P, half * PACK], BF16, name=f"x_bf{u}", align_bytes=64) for u in range(2)]
+        for u in range(2):
+            interleave(nc.vector.tensor_copy, x_bf[u], picked, slice(u * half, (u + 1) * half))
+        for u in range(2):
+            quantize(x_mx, slice(u * half, (u + 1) * half), x_bf[u][:])
+
+        w2_mx = mx_tiles("w2", H)
+        lo = deal(nc.vector.tensor_copy, "w2", 0, 2)
+        hi = deal(nc.scalar.copy, "w2", 2, 2)
+        quantize_w(w2_mx, lo, 0, 2, 2)
+        quantize_w(w2_mx, hi, 2, 2, 2)
+
+        h_mx = mx_tiles("h", S)
+        h_bf = []
+        for b in range(S // BLK):
+            cols = slice(b * BLK, (b + 1) * BLK)
+            bank = ps.tile([P, PACK, BLK], F32, name=f"h_bank{b}")
+            for t in range(PACK):
+                matmul(bank[:, t, :], w2_mx, t, x_mx, cols, True, True)
+            dst = sb.tile([P, BLK * PACK], BF16, name=f"h_bf{b}", align_bytes=64)
+            nc.scalar.activation(dst[:].rearrange("p (n t) -> p n t", t=PACK),
+                                 bank[:].rearrange("p t n -> p n t"), ACT.Relu)
+            h_bf.append(dst)
+
+        w1_mx = mx_tiles("w1", H)
+        whole = deal(nc.vector.tensor_copy, "w1", 0, PACK)
+        quantize(h_mx, slice(0, BLK), h_bf[0][:])
+        quantize(h_mx, slice(BLK, 2 * BLK), h_bf[1][:])
+        quantize_w(w1_mx, whole, 0, PACK, PACK)
+        quantize(h_mx, slice(2 * BLK, 3 * BLK), h_bf[2][:])
+        quantize(h_mx, slice(3 * BLK, 4 * BLK), h_bf[3][:])
+
+        banks = [ps.tile([P, S], F32, name=f"o_bank{t}") for t in range(PACK)]
+        for t in range(PACK):
+            matmul(banks[t][:], w1_mx, t, x_mx, slice(0, S), True, False)
+
+        w3_mx = mx_tiles("w3", H)
+        lo = deal(nc.vector.tensor_copy, "w3", 0, 2)
+        hi = deal(nc.scalar.copy, "w3", 2, 2)
+        quantize_w(w3_mx, lo, 0, 2, 1)
+        quantize_w(w3_mx, hi, 2, 2, 1)
+
+        res = sb.tile([P, PACK, S], F32, name="res")
+        out_rows = out_0.rearrange("(p t) n -> p t n", t=PACK)
+        for t in range(PACK):
+            matmul(banks[t][:], w3_mx, t, h_mx, slice(0, S), False, True)
+            if t % 2 == 0:
+                nc.scalar.copy(res[:, t, :], banks[t][:])
+            else:
+                nc.vector.tensor_copy(res[:, t, :], banks[t][:])
+            nc.sync.dma_start(out_rows[:, t, :], res[:, t, :])
+
+        o_mx = mx_tiles("o", S)
+        words = out_1[0].rearrange("p c r -> p (c r)").bitcast(I32)
+        o_bf = sb.tile([P, S * PACK], BF16, name="o_bf", align_bytes=64)
+        for copy, c0, c1 in ((nc.vector.tensor_copy, 0, 256), (nc.scalar.copy, 384, 512), (nc.vector.tensor_copy, 256, 384)):
+            interleave(copy, o_bf[:, c0 * PACK:c1 * PACK], res, slice(c0, c1))
+        for u in range(2):
+            cols = slice(u * half, (u + 1) * half)
+            quantize(o_mx, cols, o_bf[:, u * half * PACK:(u + 1) * half * PACK])
+            nc.sync.dma_start(words[:, cols], o_mx[0][:, cols].bitcast(I32))
+        scale_rows = out_2[0].bitcast(I32)
+        for q in range(4):
+            eng = nc.sync if q % 2 == 0 else nc.scalar
+            eng.dma_start(scale_rows[4 * q:4 * q + 4, :], o_mx[1][32 * q:32 * q + 4, :].bitcast(I32))

@@ -26,15 +26,18 @@ def tile_picked_lora_relu_lo_kernel(tc, xT, w1, w2, w3, offs, out_0, out_1, out_
         ps = ctx.enter_context(tc.psum_pool(name="ps", bufs=1))
 
         offsets = sb.tile([P, S // 16], U16, name="offsets")
-        nc.sync.dma_start(offsets[:], offs)
         x_rows = xT.rearrange("(p j) t -> p j t", j=PACK)
         x_raw = [sb.tile([P, T], F32, name=f"x_raw{j}") for j in range(PACK)]
         for j in range(PACK):
             nc.sync.dma_start(x_raw[j][:], x_rows[:, j, :])
+            if j == 0:
+                nc.sync.dma_start(offsets[:], offs)
         w_raw = {}
         for name, w in (("w2", w2), ("w1", w1), ("w3", w3)):
-            w_raw[name] = sb.tile([P, PACK, H], F32, name=name + "_raw")
+            w_raw[name] = sb.tile([P, PACK, H], F32, name=name + "_raw", tag=name + "_raw", align_bytes=64)
             nc.sync.dma_start(w_raw[name][:], w.rearrange("(p j) c -> p j c", j=PACK))
+
+        w_bf = {name: sb.tile([P, H * PACK], BF16, name=name + "_bf", align_bytes=64) for name in w_raw}
 
         def mx_tiles(name, width):
             return (sb.tile([P, width], U32, name=name + "_codes", align_bytes=64),
@@ -53,71 +56,86 @@ def tile_picked_lora_relu_lo_kernel(tc, xT, w1, w2, w3, offs, out_0, out_1, out_
             copy(dst[:].rearrange("p (c i j) -> p c j i", i=4, j=PACK),
                  src[:, :, cols].rearrange("p j (c i) -> p c j i", i=4))
 
-        def deal(copy, name, t0, nt):
-            dst = sb.tile([P, nt * P * PACK], BF16, name=f"{name}_bf{t0}", align_bytes=64)
-            copy(dst[:].rearrange("p (t m j) -> p m j t", t=nt, j=PACK),
-                 w_raw[name][:].rearrange("p j (m t) -> p m j t", t=PACK)[:, :, :, t0:t0 + nt])
+        def deal(copy, name, t0, nt, m0=0, m1=P):
+            dst = w_bf[name][:, t0 * P * PACK:(t0 + nt) * P * PACK]
+            copy(dst.rearrange("p (t m j) -> p m j t", t=nt, j=PACK)[:, m0:m1],
+                 w_raw[name][:].rearrange("p j (m t) -> p m j t", t=PACK)[:, m0:m1, :, t0:t0 + nt])
             return dst
+
+        def deal_upper(name):
+            dst = sb.tile([P, 2, P // 2 * PACK], BF16, name=name + "_upper", align_bytes=64)
+            nc.scalar.copy(dst[:].rearrange("p t (m j) -> p m j t", j=PACK),
+                           w_raw[name][:].rearrange("p j (m t) -> p m j t", t=PACK)[:, P // 2:, :, 2:])
+            return dst
+
+        def quantize_split(mx, name, upper, t):
+            c0 = t * P
+            quantize(mx, slice(c0, c0 + P // 2), w_bf[name][:, c0 * PACK:(c0 + P // 2) * PACK])
+            quantize(mx, slice(c0 + P // 2, c0 + P), upper[:, t - 2, :])
 
         def quantize_w(mx, dst, t0, nt, step):
             for t in range(0, nt, step):
                 quantize(mx, slice((t0 + t) * P, (t0 + t + step) * P), dst[:, t * P * PACK:(t + step) * P * PACK])
 
         picked = sb.tile([P, PACK, S], BF16, name="picked")
-        for j in range(PACK - 1):
-            nc.scalar.activation(picked[:, j, :], x_raw[j][:].indirect(offsets[:]), ACT.Copy)
         half = S // 2
-        j = PACK - 1
-        nc.vector.tensor_copy(picked[:, j, :half], x_raw[j][:].indirect(offsets[:, :half // 16]))
-        nc.scalar.activation(picked[:, j, half:], x_raw[j][:].indirect(offsets[:, half // 16:]), ACT.Copy)
+        on_vector = (384, 512, 0, 256)
+        for j in range(PACK):
+            cut = on_vector[j]
+            if cut > 0:
+                nc.vector.tensor_copy(picked[:, j, :cut], x_raw[j][:].indirect(offsets[:, :cut // 16]))
+            if cut < S:
+                nc.scalar.activation(picked[:, j, cut:], x_raw[j][:].indirect(offsets[:, cut // 16:]), ACT.Copy)
 
         x_mx = mx_tiles("x", S)
-        x_bf = [sb.tile([P, half * PACK], BF16, name=f"x_bf{u}", align_bytes=64) for u in range(2)]
-        for u in range(2):
-            interleave(nc.vector.tensor_copy, x_bf[u], picked, slice(u * half, (u + 1) * half))
-        for u in range(2):
-            quantize(x_mx, slice(u * half, (u + 1) * half), x_bf[u][:])
+        x_bf = sb.tile([P, S * PACK], BF16, name="x_bf", align_bytes=64)
+        for copy, c0, c1 in ((nc.vector.tensor_copy, 0, 336), (nc.scalar.copy, 336, S)):
+            interleave(copy, x_bf[:, c0 * PACK:c1 * PACK], picked, slice(c0, c1))
+        quantize(x_mx, slice(0, S), x_bf[:])
 
         w2_mx = mx_tiles("w2", H)
+        upper = deal_upper("w2")
+        deal(nc.vector.tensor_copy, "w2", 2, 2, 0, P // 2)
         lo = deal(nc.vector.tensor_copy, "w2", 0, 2)
-        hi = deal(nc.scalar.copy, "w2", 2, 2)
+        quantize_split(w2_mx, "w2", upper, 2)
+        quantize_split(w2_mx, "w2", upper, 3)
         quantize_w(w2_mx, lo, 0, 2, 2)
-        quantize_w(w2_mx, hi, 2, 2, 2)
 
-        h_mx = mx_tiles("h", S)
-        h_bf = []
+        h_bf = sb.tile([P, S * PACK], BF16, name="h_bf", align_bytes=64)
         for b in range(S // BLK):
             cols = slice(b * BLK, (b + 1) * BLK)
             bank = ps.tile([P, PACK, BLK], F32, name=f"h_bank{b}")
             for t in range(PACK):
                 matmul(bank[:, t, :], w2_mx, t, x_mx, cols, True, True)
-            dst = sb.tile([P, BLK * PACK], BF16, name=f"h_bf{b}", align_bytes=64)
-            nc.scalar.activation(dst[:].rearrange("p (n t) -> p n t", t=PACK),
+            dst = h_bf[:, b * BLK * PACK:(b + 1) * BLK * PACK]
+            nc.scalar.activation(dst.rearrange("p (n t) -> p n t", t=PACK),
                                  bank[:].rearrange("p t n -> p n t"), ACT.Relu)
-            h_bf.append(dst)
 
         w1_mx = mx_tiles("w1", H)
-        whole = deal(nc.vector.tensor_copy, "w1", 0, PACK)
-        quantize(h_mx, slice(0, BLK), h_bf[0][:])
-        quantize(h_mx, slice(BLK, 2 * BLK), h_bf[1][:])
-        quantize_w(w1_mx, whole, 0, PACK, PACK)
-        quantize(h_mx, slice(2 * BLK, 3 * BLK), h_bf[2][:])
-        quantize(h_mx, slice(3 * BLK, 4 * BLK), h_bf[3][:])
-
         banks = [ps.tile([P, S], F32, name=f"o_bank{t}") for t in range(PACK)]
-        for t in range(PACK):
-            matmul(banks[t][:], w1_mx, t, x_mx, slice(0, S), True, False)
+        parts = [deal(nc.vector.tensor_copy, "w1", 2 * u, 2) for u in range(2)]
+        for u in range(2):
+            quantize_w(w1_mx, parts[u], 2 * u, 2, 2)
+            for t in range(2 * u, 2 * u + 2):
+                matmul(banks[t][:], w1_mx, t, x_mx, slice(0, S), True, False)
+
+        h_first = mx_tiles("h_first", half)
+        quantize(h_first, slice(0, half), h_bf[:, :half * PACK])
 
         w3_mx = mx_tiles("w3", H)
-        lo = deal(nc.vector.tensor_copy, "w3", 0, 2)
-        hi = deal(nc.scalar.copy, "w3", 2, 2)
-        quantize_w(w3_mx, lo, 0, 2, 1)
-        quantize_w(w3_mx, hi, 2, 2, 1)
+        parts = [deal(nc.vector.tensor_copy, "w3", 2 * u, 2) for u in range(2)]
+        quantize(w3_mx, slice(0, P), parts[0][:, :P * PACK])
+        h_second = (sb.tile([P, half], U32, name="h_second_codes", tag="w3_raw", align_bytes=64),
+                    sb.tile([P, half], U8, name="h_second_scales", align_bytes=64))
+        quantize(h_second, slice(0, half), h_bf[:, half * PACK:])
+        quantize(w3_mx, slice(P, 2 * P), parts[0][:, P * PACK:])
+        quantize_w(w3_mx, parts[1], 2, 2, 1)
 
         res = sb.tile([P, PACK, S], F32, name="res")
         out_rows = out_0.rearrange("(p t) n -> p t n", t=PACK)
         for t in range(PACK):
-            matmul(banks[t][:], w3_mx, t, h_mx, slice(0, S), False, True)
+            matmul(banks[t][:, :half], w3_mx, t, h_first, slice(0, half), False, False)
+            matmul(banks[t][:, half:], w3_mx, t, h_second, slice(0, half), False, True)
             if t % 2 == 0:
                 nc.scalar.copy(res[:, t, :], banks[t][:])
             else:
@@ -127,7 +145,7 @@ def tile_picked_lora_relu_lo_kernel(tc, xT, w1, w2, w3, offs, out_0, out_1, out_
         o_mx = mx_tiles("o", S)
         words = out_1[0].rearrange("p c r -> p (c r)").bitcast(I32)
         o_bf = sb.tile([P, S * PACK], BF16, name="o_bf", align_bytes=64)
-        for copy, c0, c1 in ((nc.vector.tensor_copy, 0, 256), (nc.scalar.copy, 384, 512), (nc.vector.tensor_copy, 256, 384)):
+        for copy, c0, c1 in ((nc.vector.tensor_copy, 0, 256), (nc.scalar.copy, 336, 512), (nc.vector.tensor_copy, 256, 336)):
             interleave(copy, o_bf[:, c0 * PACK:c1 * PACK], res, slice(c0, c1))
         for u in range(2):
             cols = slice(u * half, (u + 1) * half)

@@ -123,13 +123,16 @@ def tile_picked_lora_relu_lo_kernel(tc, xT, w1, w2, w3, offs, out_0, out_1, out_
         quantize(h_first, slice(0, half), h_bf[:, :half * PACK])
 
         w3_mx = mx_tiles("w3", H)
-        parts = [deal(nc.vector.tensor_copy, "w3", 2 * u, 2) for u in range(2)]
-        quantize(w3_mx, slice(0, P), parts[0][:, :P * PACK])
+        lo = deal(nc.vector.tensor_copy, "w3", 0, 2)
+        deal(nc.vector.tensor_copy, "w3", 2, 2, 0, P // 2)
+        upper = deal_upper("w3")
+        quantize(w3_mx, slice(0, P), lo[:, :P * PACK])
+        quantize(w3_mx, slice(P, 2 * P), lo[:, P * PACK:])
         h_second = (sb.tile([P, half], U32, name="h_second_codes", tag="w3_raw", align_bytes=64),
                     sb.tile([P, half], U8, name="h_second_scales", align_bytes=64))
         quantize(h_second, slice(0, half), h_bf[:, half * PACK:])
-        quantize(w3_mx, slice(P, 2 * P), parts[0][:, P * PACK:])
-        quantize_w(w3_mx, parts[1], 2, 2, 1)
+        quantize_split(w3_mx, "w3", upper, 2)
+        quantize_split(w3_mx, "w3", upper, 3)
 
         res = sb.tile([P, PACK, S], F32, name="res")
         out_rows = out_0.rearrange("(p t) n -> p t n", t=PACK)

from contextlib import ExitStack

import concourse.mybir as mybir

K, T, S, H = 512, 1024, 512, 512
FLOPS = 3 * 2 * K * H * S

F32 = mybir.dt.float32
BF16 = mybir.dt.bfloat16
I32 = mybir.dt.int32
U32 = mybir.dt.uint32
U16 = mybir.dt.uint16
U8 = mybir.dt.uint8
FP8X4 = mybir.dt.float8_e4m3fn_x4
ACT = mybir.ActivationFunctionType

P = 128
PACK = 4
BLK = 128


def tile_picked_lora_relu_lo_kernel(tc, xT, w1, w2, w3, offs, out_0, out_1, out_2):
    nc = tc.nc
    with ExitStack() as ctx:
        sb = ctx.enter_context(tc.tile_pool(name="sb", bufs=1))
        ps = ctx.enter_context(tc.psum_pool(name="ps", bufs=1))

        offsets = sb.tile([P, S // 16], U16, name="offsets")
        x_rows = xT.rearrange("(p j) t -> p j t", j=PACK)
        x_raw = [sb.tile([P, T], F32, name=f"x_raw{j}") for j in range(PACK)]
        for j in range(PACK):
            nc.sync.dma_start(x_raw[j][:], x_rows[:, j, :])
            if j == 0:
                nc.sync.dma_start(offsets[:], offs)
        w_raw = {}
        for name, w in (("w2", w2), ("w1", w1), ("w3", w3)):
            w_raw[name] = sb.tile([P, PACK, H], F32, name=name + "_raw", tag=name + "_raw", align_bytes=64)
            nc.sync.dma_start(w_raw[name][:], w.rearrange("(p j) c -> p j c", j=PACK))

        w_bf = {name: sb.tile([P, H * PACK], BF16, name=name + "_bf", align_bytes=64) for name in w_raw}

        def mx_tiles(name, width):
            return (sb.tile([P, width], U32, name=name + "_codes", align_bytes=64),
                    sb.tile([P, width], U8, name=name + "_scales", align_bytes=64))

        def quantize(mx, cols, src):
            nc.vector.quantize_mx(out=mx[0][:, cols].bitcast(FP8X4), scales=mx[1][:, cols], in_=src)

        def matmul(out, w_mx, t, a_mx, cols, start, stop):
            wc = slice(t * P, (t + 1) * P)
            nc.tensor.matmul_mx(out=out, lhsT=w_mx[0][:, wc].bitcast(FP8X4), lhsT_scale=w_mx[1][:, wc],
                                rhs=a_mx[0][:, cols].bitcast(FP8X4), rhs_scale=a_mx[1][:, cols],
                                start=start, stop=stop)

        def interleave(copy, dst, src, cols):
            copy(dst[:].rearrange("p (c i j) -> p c j i", i=4, j=PACK),
                 src[:, :, cols].rearrange("p j (c i) -> p c j i", i=4))

        def deal(copy, name, t0, nt, m0=0, m1=P):
            dst = w_bf[name][:, t0 * P * PACK:(t0 + nt) * P * PACK]
            copy(dst.rearrange("p (t m j) -> p m j t", t=nt, j=PACK)[:, m0:m1],
                 w_raw[name][:].rearrange("p j (m t) -> p m j t", t=PACK)[:, m0:m1, :, t0:t0 + nt])
            return dst

        def deal_upper(name):
            dst = sb.tile([P, 2, P // 2 * PACK], BF16, name=name + "_upper", align_bytes=64)
            nc.scalar.copy(dst[:].rearrange("p t (m j) -> p m j t", j=PACK),
                           w_raw[name][:].rearrange("p j (m t) -> p m j t", t=PACK)[:, P // 2:, :, 2:])
            return dst

        def quantize_split(mx, name, upper, t):
            c0 = t * P
            quantize(mx, slice(c0, c0 + P // 2), w_bf[name][:, c0 * PACK:(c0 + P // 2) * PACK])
            quantize(mx, slice(c0 + P // 2, c0 + P), upper[:, t - 2, :])

        def quantize_w(mx, dst, t0, nt, step):
            for t in range(0, nt, step):
                quantize(mx, slice((t0 + t) * P, (t0 + t + step) * P), dst[:, t * P * PACK:(t + step) * P * PACK])

        picked = sb.tile([P, PACK, S], BF16, name="picked")
        half = S // 2
        on_vector = (384, 512, 0, 256)
        for j in range(PACK):
            cut = on_vector[j]
            if cut > 0:
                nc.vector.tensor_copy(picked[:, j, :cut], x_raw[j][:].indirect(offsets[:, :cut // 16]))
            if cut < S:
                nc.scalar.activation(picked[:, j, cut:], x_raw[j][:].indirect(offsets[:, cut // 16:]), ACT.Copy)

        x_mx = mx_tiles("x", S)
        x_bf = sb.tile([P, S * PACK], BF16, name="x_bf", align_bytes=64)
        for copy, c0, c1 in ((nc.vector.tensor_copy, 0, 336), (nc.scalar.copy, 336, S)):
            interleave(copy, x_bf[:, c0 * PACK:c1 * PACK], picked, slice(c0, c1))
        quantize(x_mx, slice(0, S), x_bf[:])

        w2_mx = mx_tiles("w2", H)
        upper = deal_upper("w2")
        deal(nc.vector.tensor_copy, "w2", 2, 2, 0, P // 2)
        lo = deal(nc.vector.tensor_copy, "w2", 0, 2)
        quantize_split(w2_mx, "w2", upper, 2)
        quantize_split(w2_mx, "w2", upper, 3)
        quantize_w(w2_mx, lo, 0, 2, 2)

        h_bf = sb.tile([P, S * PACK], BF16, name="h_bf", align_bytes=64)
        for b in range(S // BLK):
            cols = slice(b * BLK, (b + 1) * BLK)
            bank = ps.tile([P, PACK, BLK], F32, name=f"h_bank{b}")
            for t in range(PACK):
                matmul(bank[:, t, :], w2_mx, t, x_mx, cols, True, True)
            dst = h_bf[:, b * BLK * PACK:(b + 1) * BLK * PACK]
            nc.scalar.activation(dst.rearrange("p (n t) -> p n t", t=PACK),
                                 bank[:].rearrange("p t n -> p n t"), ACT.Relu)

        w1_mx = mx_tiles("w1", H)
        banks = [ps.tile([P, S], F32, name=f"o_bank{t}") for t in range(PACK)]
        parts = [deal(nc.vector.tensor_copy, "w1", 2 * u, 2) for u in range(2)]
        for u in range(2):
            quantize_w(w1_mx, parts[u], 2 * u, 2, 2)
            for t in range(2 * u, 2 * u + 2):
                matmul(banks[t][:], w1_mx, t, x_mx, slice(0, S), True, False)

        h_first = mx_tiles("h_first", half)
        quantize(h_first, slice(0, half), h_bf[:, :half * PACK])

        w3_mx = mx_tiles("w3", H)
        lo = deal(nc.vector.tensor_copy, "w3", 0, 2)
        deal(nc.vector.tensor_copy, "w3", 2, 2, 0, P // 2)
        upper = deal_upper("w3")
        quantize(w3_mx, slice(0, P), lo[:, :P * PACK])
        quantize(w3_mx, slice(P, 2 * P), lo[:, P * PACK:])
        h_second = (sb.tile([P, half], U32, name="h_second_codes", tag="w3_raw", align_bytes=64),
                    sb.tile([P, half], U8, name="h_second_scales", align_bytes=64))
        quantize(h_second, slice(0, half), h_bf[:, half * PACK:])
        quantize_split(w3_mx, "w3", upper, 2)
        quantize_split(w3_mx, "w3", upper, 3)

        res = sb.tile([P, PACK, S], F32, name="res")
        out_rows = out_0.rearrange("(p t) n -> p t n", t=PACK)
        for t in range(PACK):
            matmul(banks[t][:, :half], w3_mx, t, h_first, slice(0, half), False, False)
            matmul(banks[t][:, half:], w3_mx, t, h_second, slice(0, half), False, True)
            if t % 2 == 0:
                nc.scalar.copy(res[:, t, :], banks[t][:])
            else:
                nc.vector.tensor_copy(res[:, t, :], banks[t][:])
            nc.sync.dma_start(out_rows[:, t, :], res[:, t, :])

        o_mx = mx_tiles("o", S)
        words = out_1[0].rearrange("p c r -> p (c r)").bitcast(I32)
        o_bf = sb.tile([P, S * PACK], BF16, name="o_bf", align_bytes=64)
        for copy, c0, c1 in ((nc.vector.tensor_copy, 0, 256), (nc.scalar.copy, 336, 512), (nc.vector.tensor_copy, 256, 336)):
            interleave(copy, o_bf[:, c0 * PACK:c1 * PACK], res, slice(c0, c1))
        for u in range(2):
            cols = slice(u * half, (u + 1) * half)
            quantize(o_mx, cols, o_bf[:, u * half * PACK:(u + 1) * half * PACK])
            nc.sync.dma_start(words[:, cols], o_mx[0][:, cols].bitcast(I32))
        scale_rows = out_2[0].bitcast(I32)
        for q in range(4):
            eng = nc.sync if q % 2 == 0 else nc.scalar
            eng.dma_start(scale_rows[4 * q:4 * q + 4, :], o_mx[1][32 * q:32 * q + 4, :].bitcast(I32))
